import numpy as np
import ml_dtypes


def mxq(x, axis, fmt="e4m3"):
    dtype, down = {"e4m3": (ml_dtypes.float8_e4m3fn, 7), "e5m2": (ml_dtypes.float8_e5m2, 14)}[fmt]
    v = np.moveaxis(np.asarray(x, np.float32).astype(ml_dtypes.bfloat16).astype(np.float64), axis, -1)
    blocks = v.reshape(v.shape[:-1] + (-1, 32))
    amax = np.abs(blocks).max(-1, keepdims=True)
    byte = np.maximum(np.where(amax > 0, np.frexp(amax)[1] - 1 + 127, 0) - down, 1)
    scale = np.exp2(byte - 127.0)
    codes = (blocks / scale).astype(np.float32).astype(dtype).astype(np.float64)
    return np.moveaxis((codes * scale).reshape(v.shape), -1, axis)


WIDE = False


def mx_kscale(k):
    if not WIDE:
        return np.ones(k)
    levels = np.array([10, -10, 5, -5, 0])
    if k % 512:
        return np.exp2(np.random.permutation(np.resize(levels, k // 32))).repeat(32)
    a = np.empty((k // 512, 16))
    for p in range(k // 512):
        a[p, :8] = np.random.permutation(np.resize(levels, 8))
        for g in range(8):
            far = levels[np.abs(levels - a[p, g]) >= 10]
            a[p, g + 8] = far[np.random.randint(len(far))]
    return np.exp2(a.ravel()).repeat(32)


def f64(x):
    return np.asarray(x).astype(np.float64)


def striped(idx):
    return np.tile(idx.reshape(-1, 16).T, (8, 1)).astype(np.uint16)


def unstriped(offs):
    return offs[:16].T.reshape(-1).astype(np.int64)


def striped8(idx):
    return np.concatenate([x.reshape(-1, 16).T for x in idx]).astype(np.uint16)


def runs(offs, k):
    lists = np.stack([offs[16 * r : 16 * r + 16].T.reshape(-1) for r in range(8)]).astype(np.int64)
    return lists[np.arange(k) % 512 // 64]


def pack_weight(w):
    k, n = w.shape
    w = f64(np.asarray(w, np.float32).astype(ml_dtypes.bfloat16)).reshape(k // 32, 32, n)
    amax = np.abs(w).max(1)
    byte = np.clip(np.where(amax > 0, np.frexp(amax)[1] - 1 + 127 - 7, 1), 1, 254)
    scaled = (w * np.exp2(127.0 - byte)[:, None, :]).reshape(k, n).astype(np.float32)
    words = np.ascontiguousarray(scaled.reshape(k // 512, 128, 4, n).transpose(0, 1, 3, 2)).astype(ml_dtypes.float8_e4m3fn).view(np.uint8)
    return words, np.ascontiguousarray(byte.astype(np.uint8).reshape(k // 512, 16, n))


def unpack_weight(words, scales):
    g, p, n, _ = words.shape
    vals = np.ascontiguousarray(words).view(ml_dtypes.float8_e4m3fn).astype(np.float64) * np.repeat(np.exp2(scales.astype(np.float64) - 127.0), 8, axis=1)[..., None]
    return vals.transpose(0, 1, 3, 2).reshape(g * 512, n)


def relu(v):
    return np.maximum(v, 0.0)


K, T, S, N, H = 512, 2048, 512, 512, 512


def setup_inputs():
    n = np.random.standard_normal
    s = mx_kscale(K)[:, None]
    u = mx_kscale(H)
    packed_xT = pack_weight(n((K, T)) * s)
    return {
        "x_words": packed_xT[0],
        "x_scales": packed_xT[1],
        "w1": (n((K, H)) / np.sqrt(K) / s).astype(np.float32),
        "gn": (np.random.uniform(0.5, 1.5, (H, 1)) * u[:, None]).astype(np.float32),
        "w2": (n((H, H)) / np.sqrt(H) / u[:, None]).astype(np.float32),
        "res": n((N, S)).astype(np.float32),
        "w3": (n((H, N)) / np.sqrt(H) / u[:, None]).astype(np.float32),
        "offs": striped(np.random.permutation(T)[:S]),
        "lf": striped8(np.stack([np.random.permutation(S) for _ in range(8)])),
        "rt": striped8(np.stack([np.random.permutation(S) for _ in range(8)])),
        "mv": striped8(np.stack([np.random.permutation(S) for _ in range(8)])),
    }


def reference(x_words, x_scales, w1, gn, w2, res, w3, offs, lf, rt, mv):
    xq = unpack_weight(x_words, x_scales)[:, unstriped(offs)]
    y = mxq(f64(w1), 0, "e4m3").T @ xq
    a = y - (y[np.arange(H)[:, None], runs(lf, H)])
    b = y[np.arange(H)[:, None], runs(rt, H)] - y
    z = f64(gn) * ((2.0 * relu(a * b)) / (np.abs(a) + np.abs(b) + 0.1))
    h = np.tanh(mxq(f64(w2), 0, "e4m3").T @ mxq(z, 0, "e4m3"))
    z2 = f64(gn) * (h[np.arange(H)[:, None], runs(mv, H)])
    return f64(res) + (mxq(f64(w3), 0, "e4m3").T @ mxq(z2, 0, "e4m3"))

@@ -1,0 +1,198 @@
+from contextlib import ExitStack
+
+import concourse.mybir as mybir
+from concourse.masks import make_identity
+
+F32, BF16 = mybir.dt.float32, mybir.dt.bfloat16
+I32, U32, U16, U8 = mybir.dt.int32, mybir.dt.uint32, mybir.dt.uint16, mybir.dt.uint8
+FP8X4 = mybir.dt.float8_e4m3fn_x4
+ALU = mybir.AluOpType
+ACT = mybir.ActivationFunctionType
+
+P = 128
+PACK = 4
+K, T, S = 512, 2048, 512
+HALF = S // 2
+FLOPS = 3 * 2 * 512 * 512 * 512
+
+
+def tile_picked_vanleer2_none_p_kernel(
+    tc, x_words, x_scales, w1, gn, w2, res, w3, offs, lf, rt, mv, out
+):
+    nc = tc.nc
+    with ExitStack() as ctx:
+        sb = ctx.enter_context(tc.tile_pool(name="sb", bufs=1))
+        ps = ctx.enter_context(tc.psum_pool(name="ps", bufs=1))
+
+        def sbuf(name, shape, dtype):
+            return sb.tile(shape, dtype, name=name, align_bytes=64)
+
+        def bank(tag, name):
+            return ps.tile([P, S], F32, name=name, tag=tag)
+
+        lists = {n: sb.tile([P, S // 16], U16, name=n + "_list") for n in ("offs", "lf", "rt", "mv")}
+        w_raw = [sbuf("w_raw%d" % i, [P, PACK, K], F32) for i in range(3)]
+        w_bf = [sbuf("w_bf%d" % i, [P, PACK * K], BF16) for i in range(3)]
+        w_code = [sbuf("w_code%d" % i, [P, K], U32) for i in range(3)]
+        w_scale = [sbuf("w_scale%d" % i, [P, K], U8) for i in range(3)]
+        x_all = sbuf("x_all", [P, T], I32)
+        xs_all = sbuf("xs_all", [P, T], U8)
+        gain = sbuf("gain", [P, PACK], F32)
+        res_sb = sbuf("res_sb", [P, PACK, S], F32)
+
+        nc.gpsimd.memset(xs_all[:].bitcast(I32), 0)
+        nc.sync.dma_start(w_raw[0][:], w1.rearrange("(p j) c -> p j c", j=PACK))
+        nc.sync.dma_start(lists["offs"][:], offs)
+        nc.sync.dma_start(x_all[:], x_words[0].rearrange("p n t -> p (n t)").bitcast(I32))
+        for q in range(4):
+            nc.scalar.dma_start(xs_all[32 * q : 32 * q + 4, :].bitcast(I32), x_scales[0, 4 * q : 4 * q + 4, :].bitcast(I32))
+        nc.sync.dma_start(lists["lf"][:], lf)
+        nc.sync.dma_start(lists["rt"][:], rt)
+        nc.sync.dma_start(w_raw[1][:], w2.rearrange("(p j) c -> p j c", j=PACK))
+        nc.sync.dma_start(gain[:], gn.rearrange("(p t) o -> p (t o)", t=PACK))
+        nc.sync.dma_start(lists["mv"][:], mv)
+        nc.sync.dma_start(w_raw[2][:], w3.rearrange("(p j) c -> p j c", j=PACK))
+        nc.sync.dma_start(res_sb[:], res.rearrange("(t p) n -> p t n", p=P))
+
+        ident = sbuf("ident", [P, P], F32)
+        make_identity(nc, ident[:])
+
+        y = [sbuf("y%d" % t, [P, 2 * S], F32) for t in range(PACK)]
+        ny = [sbuf("ny%d" % t, [P, 2 * S], F32) for t in range(PACK)]
+        for t in range(PACK):
+            nc.vector.memset(y[t][:, S:], 0.0)
+            nc.vector.memset(ny[t][:, S:], 0.0)
+
+        def deal(engine_copy, i, m0, m1):
+            dst = w_bf[i][:].rearrange("p (t m j) -> p m j t", t=PACK, j=PACK)
+            src = w_raw[i][:].rearrange("p j (m t) -> p m j t", t=PACK)
+            engine_copy(dst[:, m0:m1], src[:, m0:m1])
+
+        def quantise(codes, scales, values):
+            nc.vector.quantize_mx(out=codes.bitcast(FP8X4), scales=scales, in_=values)
+
+        def product(dst, i, t, codes, scales):
+            cols = slice(P * t, P * (t + 1))
+            nc.tensor.matmul_mx(
+                out=dst, lhsT=w_code[i][:, cols].bitcast(FP8X4), lhsT_scale=w_scale[i][:, cols],
+                rhs=codes.bitcast(FP8X4), rhs_scale=scales, start=True, stop=True,
+            )
+
+        deal(nc.vector.tensor_copy, 0, 0, 80)
+        deal(nc.scalar.copy, 0, 80, 128)
+        quantise(w_code[0][:], w_scale[0][:], w_bf[0][:])
+
+        x_code = sbuf("x_code", [P, S], U32)
+        x_scale = sbuf("x_scale", [P, S], U8)
+        nc.vector.tensor_copy(x_scale[:], xs_all[:].indirect(lists["offs"][:]))
+        halves = [slice(0, HALF), slice(HALF, S)]
+        for half in range(2):
+            nc.vector.tensor_copy(
+                x_code[:, halves[half]], x_all[:].bitcast(U32).indirect(lists["offs"][:, 16 * half : 16 * (half + 1)])
+            )
+
+        for pair in range(2):
+            y_ps = [bank("A%d" % (2 * pair + half), "y_ps%d%d" % (pair, half)) for half in range(2)]
+            for half in range(2):
+                for u in range(2):
+                    product(y_ps[half][:, halves[u]], 0, 2 * pair + u, x_code[:, halves[half]], x_scale[:, halves[half]])
+            for u in range(2):
+                t = 2 * pair + u
+                for half in range(2):
+                    nc.scalar.copy(y[t][:, halves[half]], y_ps[half][:, halves[u]])
+                    if t == 0:
+                        nc.vector.tensor_scalar(ny[t][:, halves[half]], y[t][:, halves[half]], -1.0, None, ALU.mult)
+                    else:
+                        nc.scalar.activation(ny[t][:, halves[half]], y_ps[half][:, halves[u]], ACT.Copy, scale=-1.0)
+
+        a = sbuf("a", [P, PACK, S], F32)
+        b = sbuf("b", [P, PACK, S], F32)
+        for t in range(PACK):
+            nc.vector.tensor_tensor(a[:, t, :], ny[t][:].indirect(lists["lf"][:]), y[t][:, :S], ALU.add)
+            nc.vector.tensor_tensor(b[:, t, :], y[t][:].indirect(lists["rt"][:]), ny[t][:, :S], ALU.add)
+
+        size = sbuf("size", [P, PACK, S], F32)
+        root = sbuf("root", [P, PACK, S], F32)
+        recip = sbuf("recip", [P, PACK, S], F32)
+        recip_ps = [bank("A%d" % c, "recip_ps%d" % c) for c in range(PACK)]
+        for t in range(PACK):
+            sum_ps = bank("B%d" % t, "sum_ps%d" % t)
+            for c in range(PACK):
+                cols = slice(P * c, P * (c + 1))
+                nc.tensor.matmul(sum_ps[:, cols], a[:, t, cols], ident[:], start=True, stop=False, is_transpose=True)
+                nc.tensor.matmul(sum_ps[:, cols], b[:, t, cols], ident[:], start=False, stop=True, is_transpose=True)
+            if t == PACK - 1:
+                deal(nc.scalar.copy, 1, 64, 128)
+            nc.scalar.activation(size[:, t, :], sum_ps[:], ACT.Abs)
+            nc.scalar.activation(root[:, t, :], size[:, t, :], ACT.Abs_reciprocal_sqrt, bias=0.05, scale=0.5)
+            nc.scalar.activation(recip[:, t, :], root[:, t, :], ACT.Square)
+            for c in range(PACK):
+                nc.tensor.transpose(recip_ps[c][:, P * t : P * (t + 1)], recip[:, t, P * c : P * (c + 1)], ident[:])
+
+        ab = sbuf("ab", [P, PACK, S], F32)
+        num = sbuf("num", [P, PACK, S], F32)
+        for t in range(PACK):
+            nc.vector.tensor_tensor(ab[:, t, :], a[:, t, :], b[:, t, :], ALU.mult)
+        for t in range(PACK):
+            nc.vector.tensor_scalar(num[:, t, :], ab[:, t, :], 0.0, gain[:, t : t + 1], ALU.max, ALU.mult)
+        deal(nc.vector.tensor_copy, 1, 0, 64)
+        quantise(w_code[1][:], w_scale[1][:], w_bf[1][:])
+
+        nc.scalar.copy(
+            w_bf[2][:].rearrange("p (c i j) -> p c j i", i=PACK, j=PACK),
+            w_raw[2][:].rearrange("p j (c i) -> p c j i", i=PACK),
+        )
+
+        z_bf = sbuf("z_bf", [P, PACK * S], BF16)
+        z_code = sbuf("z_code", [P, S], U32)
+        z_scale = sbuf("z_scale", [P, S], U8)
+        h = [sbuf("h%d" % t, [P, S], F32) for t in range(PACK)]
+        gh = [sbuf("gh%d" % t, [P, S], F32) for t in range(PACK)]
+        for half in range(2):
+            for c in range(2 * half, 2 * half + 2):
+                nc.vector.tensor_tensor(
+                    z_bf[:, S * c : S * (c + 1)].rearrange("p (c i t) -> p c t i", i=PACK, t=PACK),
+                    num[:, :, P * c : P * (c + 1)].rearrange("p t (c i) -> p c t i", i=PACK),
+                    recip_ps[c][:].rearrange("p (t c i) -> p c t i", t=PACK, i=PACK),
+                    ALU.mult,
+                )
+        for half in range(2):
+            cols = slice(HALF * half, HALF * (half + 1))
+            quantise(z_code[:, cols], z_scale[:, cols], z_bf[:, PACK * cols.start : PACK * cols.stop])
+            for pair in range(2):
+                h_ps = bank("B%d" % (2 * half + pair), "h_ps%d%d" % (half, pair))
+                for u in range(2):
+                    product(h_ps[:, HALF * u : HALF * (u + 1)], 1, 2 * pair + u, z_code[:, cols], z_scale[:, cols])
+                for u in range(2):
+                    t = 2 * pair + u
+                    nc.scalar.activation(h[t][:, cols], h_ps[:, HALF * u : HALF * (u + 1)], ACT.Tanh)
+                    nc.scalar.activation(gh[t][:, cols], h[t][:, cols], ACT.Copy, scale=gain[:, t : t + 1])
+        quantise(w_code[2][:], w_scale[2][:], w_bf[2][:])
+
+        moved = sbuf("moved", [P, 2, PACK, HALF], BF16)
+        z2_bf = sbuf("z2_bf", [P, PACK * S], BF16)
+        z2_code = sbuf("z2_code", [P, S], U32)
+        z2_scale = sbuf("z2_scale", [P, S], U8)
+        result = sbuf("result", [P, PACK, S], F32)
+        out_rows = out.rearrange("(t p) n -> p t n", p=P)
+        for half in range(2):
+            for t in range(PACK):
+                nc.vector.tensor_copy(moved[:, half, t, :], gh[t][:].indirect(lists["mv"][:, 16 * half : 16 * (half + 1)]))
+        for half in range(2):
+            cols = slice(HALF * half, HALF * (half + 1))
+            wide = slice(PACK * cols.start, PACK * cols.stop)
+            copy = nc.scalar.copy if half == 0 else nc.vector.tensor_copy
+            copy(
+                z2_bf[:, wide].rearrange("p (c i t) -> p c t i", i=PACK, t=PACK),
+                moved[:, half].rearrange("p t (c i) -> p c t i", i=PACK),
+            )
+            quantise(z2_code[:, cols], z2_scale[:, cols], z2_bf[:, wide])
+            for pair in range(2):
+                o_ps = bank("A%d" % (2 * half + pair), "o_ps%d%d" % (half, pair))
+                for u in range(2):
+                    product(o_ps[:, HALF * u : HALF * (u + 1)], 2, 2 * pair + u, z2_code[:, cols], z2_scale[:, cols])
+                rows = slice(2 * pair, 2 * pair + 2)
+                nc.vector.tensor_tensor(
+                    result[:, rows, cols], o_ps[:].rearrange("p (u n) -> p u n", u=2), res_sb[:, rows, cols], ALU.add
+                )
+                nc.sync.dma_start(out_rows[:, rows, cols], result[:, rows, cols])

@@ -42,10 +42,10 @@ def tile_picked_vanleer2_none_p_kernel(
 
         nc.gpsimd.memset(xs_all[:].bitcast(I32), 0)
         nc.sync.dma_start(w_raw[0][:], w1.rearrange("(p j) c -> p j c", j=PACK))
+        for q in range(4):
+            nc.sync.dma_start(xs_all[32 * q : 32 * q + 4, :].bitcast(I32), x_scales[0, 4 * q : 4 * q + 4, :].bitcast(I32))
         nc.sync.dma_start(lists["offs"][:], offs)
         nc.sync.dma_start(x_all[:], x_words[0].rearrange("p n t -> p (n t)").bitcast(I32))
-        for q in range(4):
-            nc.scalar.dma_start(xs_all[32 * q : 32 * q + 4, :].bitcast(I32), x_scales[0, 4 * q : 4 * q + 4, :].bitcast(I32))
         nc.sync.dma_start(lists["lf"][:], lf)
         nc.sync.dma_start(lists["rt"][:], rt)
         nc.sync.dma_start(w_raw[1][:], w2.rearrange("(p j) c -> p j c", j=PACK))
@@ -53,6 +53,10 @@ def tile_picked_vanleer2_none_p_kernel(
         nc.sync.dma_start(lists["mv"][:], mv)
         nc.sync.dma_start(w_raw[2][:], w3.rearrange("(p j) c -> p j c", j=PACK))
         nc.sync.dma_start(res_sb[:], res.rearrange("(t p) n -> p t n", p=P))
+
+        warm = sbuf("warm", [P, 2], F32)
+        nc.vector.memset(warm[:, 0:1], 1.0)
+        nc.scalar.activation(warm[:, 1:2], warm[:, 0:1], ACT.Abs_reciprocal_sqrt)
 
         ident = sbuf("ident", [P, P], F32)
         make_identity(nc, ident[:])
@@ -111,6 +115,14 @@ def tile_picked_vanleer2_none_p_kernel(
             nc.vector.tensor_tensor(a[:, t, :], ny[t][:].indirect(lists["lf"][:]), y[t][:, :S], ALU.add)
             nc.vector.tensor_tensor(b[:, t, :], y[t][:].indirect(lists["rt"][:]), ny[t][:, :S], ALU.add)
 
+        deal(nc.scalar.copy, 1, 0, 128)
+
+        def weave_rows(c0, c1):
+            nc.scalar.copy(
+                w_bf[2][:].rearrange("p (c i j) -> p c j i", i=PACK, j=PACK)[:, c0:c1],
+                w_raw[2][:].rearrange("p j (c i) -> p c j i", i=PACK)[:, c0:c1],
+            )
+
         size = sbuf("size", [P, PACK, S], F32)
         root = sbuf("root", [P, PACK, S], F32)
         recip = sbuf("recip", [P, PACK, S], F32)
@@ -121,78 +133,115 @@ def tile_picked_vanleer2_none_p_kernel(
                 cols = slice(P * c, P * (c + 1))
                 nc.tensor.matmul(sum_ps[:, cols], a[:, t, cols], ident[:], start=True, stop=False, is_transpose=True)
                 nc.tensor.matmul(sum_ps[:, cols], b[:, t, cols], ident[:], start=False, stop=True, is_transpose=True)
-            if t == PACK - 1:
-                deal(nc.scalar.copy, 1, 64, 128)
+            if t in (1, 2):
+                weave_rows(64 * (t - 1), 64 * t)
             nc.scalar.activation(size[:, t, :], sum_ps[:], ACT.Abs)
             nc.scalar.activation(root[:, t, :], size[:, t, :], ACT.Abs_reciprocal_sqrt, bias=0.05, scale=0.5)
             nc.scalar.activation(recip[:, t, :], root[:, t, :], ACT.Square)
             for c in range(PACK):
                 nc.tensor.transpose(recip_ps[c][:, P * t : P * (t + 1)], recip[:, t, P * c : P * (c + 1)], ident[:])
 
-        ab = sbuf("ab", [P, PACK, S], F32)
+        ab = [ny[3][:, :S], ny[3][:, S:], y[3][:, :S], y[3][:, S:]]
         num = sbuf("num", [P, PACK, S], F32)
+        for pair, tile in enumerate((ny[3], y[3])):
+            rows = slice(2 * pair, 2 * pair + 2)
+            nc.vector.tensor_tensor(tile[:].rearrange("p (u n) -> p u n", u=2), a[:, rows, :], b[:, rows, :], ALU.mult)
         for t in range(PACK):
-            nc.vector.tensor_tensor(ab[:, t, :], a[:, t, :], b[:, t, :], ALU.mult)
-        for t in range(PACK):
-            nc.vector.tensor_scalar(num[:, t, :], ab[:, t, :], 0.0, gain[:, t : t + 1], ALU.max, ALU.mult)
-        deal(nc.vector.tensor_copy, 1, 0, 64)
+            nc.vector.tensor_scalar(num[:, t, :], ab[t], 0.0, gain[:, t : t + 1], ALU.max, ALU.mult)
         quantise(w_code[1][:], w_scale[1][:], w_bf[1][:])
 
-        nc.scalar.copy(
-            w_bf[2][:].rearrange("p (c i j) -> p c j i", i=PACK, j=PACK),
-            w_raw[2][:].rearrange("p j (c i) -> p c j i", i=PACK),
-        )
+        nc.scalar.activation(warm[:, 1:2], recip[:, PACK - 1, S - 1 : S], ACT.Tanh)
 
         z_bf = sbuf("z_bf", [P, PACK * S], BF16)
         z_code = sbuf("z_code", [P, S], U32)
         z_scale = sbuf("z_scale", [P, S], U8)
         h = [sbuf("h%d" % t, [P, S], F32) for t in range(PACK)]
         gh = [sbuf("gh%d" % t, [P, S], F32) for t in range(PACK)]
-        for half in range(2):
-            for c in range(2 * half, 2 * half + 2):
-                nc.vector.tensor_tensor(
-                    z_bf[:, S * c : S * (c + 1)].rearrange("p (c i t) -> p c t i", i=PACK, t=PACK),
-                    num[:, :, P * c : P * (c + 1)].rearrange("p t (c i) -> p c t i", i=PACK),
-                    recip_ps[c][:].rearrange("p (t c i) -> p c t i", t=PACK, i=PACK),
-                    ALU.mult,
-                )
-        for half in range(2):
-            cols = slice(HALF * half, HALF * (half + 1))
-            quantise(z_code[:, cols], z_scale[:, cols], z_bf[:, PACK * cols.start : PACK * cols.stop])
-            for pair in range(2):
-                h_ps = bank("B%d" % (2 * half + pair), "h_ps%d%d" % (half, pair))
-                for u in range(2):
-                    product(h_ps[:, HALF * u : HALF * (u + 1)], 1, 2 * pair + u, z_code[:, cols], z_scale[:, cols])
-                for u in range(2):
-                    t = 2 * pair + u
-                    nc.scalar.activation(h[t][:, cols], h_ps[:, HALF * u : HALF * (u + 1)], ACT.Tanh)
-                    nc.scalar.activation(gh[t][:, cols], h[t][:, cols], ACT.Copy, scale=gain[:, t : t + 1])
-        quantise(w_code[2][:], w_scale[2][:], w_bf[2][:])
+        stretches = [slice(0, 256), slice(256, 384), slice(384, 512)]
 
-        moved = sbuf("moved", [P, 2, PACK, HALF], BF16)
-        z2_bf = sbuf("z2_bf", [P, PACK * S], BF16)
+        def banks_of(tags, name, cols):
+            width = cols.stop - cols.start
+            per_bank = S // width
+            tiles = [bank(tag, name + tag) for tag in tags]
+            return [tiles[t // per_bank][:, width * (t % per_bank) : width * (t % per_bank + 1)] for t in range(PACK)], tiles
+
+        def slope(c):
+            nc.vector.tensor_tensor(
+                z_bf[:, S * c : S * (c + 1)].rearrange("p (c i t) -> p c t i", i=PACK, t=PACK),
+                num[:, :, P * c : P * (c + 1)].rearrange("p t (c i) -> p c t i", i=PACK),
+                recip_ps[c][:].rearrange("p (t c i) -> p c t i", t=PACK, i=PACK),
+                ALU.mult,
+            )
+
+        def hidden(cols, tags):
+            quantise(z_code[:, cols], z_scale[:, cols], z_bf[:, PACK * cols.start : PACK * cols.stop])
+            h_ps, unused = banks_of(tags, "h_ps", cols)
+            for t in range(PACK):
+                product(h_ps[t], 1, t, z_code[:, cols], z_scale[:, cols])
+            for t in range(PACK):
+                nc.scalar.activation(h[t][:, cols], h_ps[t], ACT.Tanh)
+                if cols.stop == S and t >= 2:
+                    nc.scalar.activation(gh[t][:], h[t][:], ACT.Copy, scale=gain[:, t : t + 1])
+
+        slope(0)
+        slope(1)
+        slope(2)
+        hidden(halves[0], ["B0", "B1"])
+        slope(3)
+        hidden(halves[1], ["B2", "B3"])
+        quantise(w_code[2][:], w_scale[2][:], w_bf[2][:])
+        for t in range(2):
+            nc.vector.tensor_scalar(gh[t][:], h[t][:], gain[:, t : t + 1], None, ALU.mult)
+
+        moved = sbuf("moved", [P, PACK * 384], BF16)
+        z2_bf = sbuf("z2_bf", [P, PACK * 384], BF16)
         z2_code = sbuf("z2_code", [P, S], U32)
         z2_scale = sbuf("z2_scale", [P, S], U8)
         result = sbuf("result", [P, PACK, S], F32)
         out_rows = out.rearrange("(t p) n -> p t n", p=P)
-        for half in range(2):
+        planes = [moved[:, :1024], moved[:, 1024:], z2_bf[:, :512]]
+        woven = [z2_bf[:, :1024], z2_bf[:, 1024:], z2_bf[:, 1024:]]
+
+        def fetch(s):
+            cols = stretches[s]
+            width = cols.stop - cols.start
             for t in range(PACK):
-                nc.vector.tensor_copy(moved[:, half, t, :], gh[t][:].indirect(lists["mv"][:, 16 * half : 16 * (half + 1)]))
-        for half in range(2):
-            cols = slice(HALF * half, HALF * (half + 1))
-            wide = slice(PACK * cols.start, PACK * cols.stop)
-            copy = nc.scalar.copy if half == 0 else nc.vector.tensor_copy
+                nc.vector.tensor_copy(
+                    planes[s][:, width * t : width * (t + 1)], gh[t][:].indirect(lists["mv"][:, cols.start // 16 : cols.stop // 16])
+                )
+
+        def weave(s, copy):
             copy(
-                z2_bf[:, wide].rearrange("p (c i t) -> p c t i", i=PACK, t=PACK),
-                moved[:, half].rearrange("p t (c i) -> p c t i", i=PACK),
+                woven[s].rearrange("p (c i t) -> p c t i", i=PACK, t=PACK),
+                planes[s].rearrange("p (t c i) -> p c t i", t=PACK, i=PACK),
             )
-            quantise(z2_code[:, cols], z2_scale[:, cols], z2_bf[:, wide])
-            for pair in range(2):
-                o_ps = bank("A%d" % (2 * half + pair), "o_ps%d%d" % (half, pair))
-                for u in range(2):
-                    product(o_ps[:, HALF * u : HALF * (u + 1)], 2, 2 * pair + u, z2_code[:, cols], z2_scale[:, cols])
-                rows = slice(2 * pair, 2 * pair + 2)
+
+        def last_product(s, tags):
+            cols = stretches[s]
+            quantise(z2_code[:, cols], z2_scale[:, cols], woven[s])
+            o_ps, tiles = banks_of(tags, "o_ps", cols)
+            for t in range(PACK):
+                product(o_ps[t], 2, t, z2_code[:, cols], z2_scale[:, cols])
+            return tiles
+
+        def finish(cols, tiles):
+            per_bank = PACK // len(tiles)
+            for i, tile in enumerate(tiles):
+                rows = slice(per_bank * i, per_bank * (i + 1))
                 nc.vector.tensor_tensor(
-                    result[:, rows, cols], o_ps[:].rearrange("p (u n) -> p u n", u=2), res_sb[:, rows, cols], ALU.add
+                    result[:, rows, cols], tile[:].rearrange("p (u n) -> p u n", u=per_bank), res_sb[:, rows, cols], ALU.add
                 )
                 nc.sync.dma_start(out_rows[:, rows, cols], result[:, rows, cols])
+
+        fetch(0)
+        weave(0, nc.scalar.copy)
+        fetch(1)
+        weave(1, nc.scalar.copy)
+        first_banks = last_product(0, ["A0", "A1"])
+        fetch(2)
+        second_banks = last_product(1, ["A2"])
+        weave(2, nc.vector.tensor_copy)
+        finish(stretches[0], first_banks)
+        third_banks = last_product(2, ["A3"])
+        finish(stretches[1], second_banks)
+        finish(stretches[2], third_banks)

@@ -32,7 +32,7 @@ def tile_picked_vanleer2_none_p_kernel(
 
         lists = {n: sb.tile([P, S // 16], U16, name=n + "_list") for n in ("offs", "lf", "rt", "mv")}
         w_raw = [sbuf("w_raw%d" % i, [P, PACK, K], F32) for i in range(3)]
-        w_bf = [sbuf("w_bf%d" % i, [P, PACK * K], BF16) for i in range(3)]
+        w_bf = [sbuf("w_bf%d" % i, [P, PACK * K], BF16) for i in range(2)]
         w_code = [sbuf("w_code%d" % i, [P, K], U32) for i in range(3)]
         w_scale = [sbuf("w_scale%d" % i, [P, K], U8) for i in range(3)]
         x_all = sbuf("x_all", [P, T], I32)
@@ -90,24 +90,21 @@ def tile_picked_vanleer2_none_p_kernel(
         x_scale = sbuf("x_scale", [P, S], U8)
         nc.vector.tensor_copy(x_scale[:], xs_all[:].indirect(lists["offs"][:]))
         halves = [slice(0, HALF), slice(HALF, S)]
-        for half in range(2):
+        stretches = [slice(0, 256), slice(256, 384), slice(384, 512)]
+        for s, cols in enumerate(halves):
             nc.vector.tensor_copy(
-                x_code[:, halves[half]], x_all[:].bitcast(U32).indirect(lists["offs"][:, 16 * half : 16 * (half + 1)])
+                x_code[:, cols], x_all[:].bitcast(U32).indirect(lists["offs"][:, cols.start // 16 : cols.stop // 16])
             )
-
-        for pair in range(2):
-            y_ps = [bank("A%d" % (2 * pair + half), "y_ps%d%d" % (pair, half)) for half in range(2)]
-            for half in range(2):
-                for u in range(2):
-                    product(y_ps[half][:, halves[u]], 0, 2 * pair + u, x_code[:, halves[half]], x_scale[:, halves[half]])
-            for u in range(2):
-                t = 2 * pair + u
-                for half in range(2):
-                    nc.scalar.copy(y[t][:, halves[half]], y_ps[half][:, halves[u]])
-                    if t == 0:
-                        nc.vector.tensor_scalar(ny[t][:, halves[half]], y[t][:, halves[half]], -1.0, None, ALU.mult)
-                    else:
-                        nc.scalar.activation(ny[t][:, halves[half]], y_ps[half][:, halves[u]], ACT.Copy, scale=-1.0)
+            part_ps = bank("B%d" % s, "part_ps%d" % s)
+            product(part_ps[:, cols], 0, 0, x_code[:, cols], x_scale[:, cols])
+            nc.scalar.copy(y[0][:, cols], part_ps[:, cols])
+        for cols in halves:
+            nc.vector.tensor_scalar(ny[0][:, cols], y[0][:, cols], -1.0, None, ALU.mult)
+        for t in range(1, PACK):
+            row_ps = bank("A%d" % t, "y_ps%d" % t)
+            product(row_ps[:], 0, t, x_code[:], x_scale[:])
+            nc.scalar.copy(y[t][:, :S], row_ps[:])
+            nc.scalar.activation(ny[t][:, :S], row_ps[:], ACT.Copy, scale=-1.0)
 
         a = sbuf("a", [P, PACK, S], F32)
         b = sbuf("b", [P, PACK, S], F32)
@@ -117,24 +114,17 @@ def tile_picked_vanleer2_none_p_kernel(
 
         deal(nc.scalar.copy, 1, 0, 128)
 
-        def weave_rows(c0, c1):
-            nc.scalar.copy(
-                w_bf[2][:].rearrange("p (c i j) -> p c j i", i=PACK, j=PACK)[:, c0:c1],
-                w_raw[2][:].rearrange("p j (c i) -> p c j i", i=PACK)[:, c0:c1],
-            )
-
         size = sbuf("size", [P, PACK, S], F32)
         root = sbuf("root", [P, PACK, S], F32)
         recip = sbuf("recip", [P, PACK, S], F32)
         recip_ps = [bank("A%d" % c, "recip_ps%d" % c) for c in range(PACK)]
         for t in range(PACK):
             sum_ps = bank("B%d" % t, "sum_ps%d" % t)
-            for c in range(PACK):
-                cols = slice(P * c, P * (c + 1))
-                nc.tensor.matmul(sum_ps[:, cols], a[:, t, cols], ident[:], start=True, stop=False, is_transpose=True)
-                nc.tensor.matmul(sum_ps[:, cols], b[:, t, cols], ident[:], start=False, stop=True, is_transpose=True)
-            if t in (1, 2):
-                weave_rows(64 * (t - 1), 64 * t)
+            for term in (a, b):
+                for c in range(PACK):
+                    cols = slice(P * c, P * (c + 1))
+                    first, last = term is a and c == 0, term is b and c == PACK - 1
+                    nc.tensor.matmul(sum_ps[:, cols], term[:, t, cols], ident[:], start=first, stop=last, is_transpose=True)
             nc.scalar.activation(size[:, t, :], sum_ps[:], ACT.Abs)
             nc.scalar.activation(root[:, t, :], size[:, t, :], ACT.Abs_reciprocal_sqrt, bias=0.05, scale=0.5)
             nc.scalar.activation(recip[:, t, :], root[:, t, :], ACT.Square)
@@ -152,12 +142,17 @@ def tile_picked_vanleer2_none_p_kernel(
 
         nc.scalar.activation(warm[:, 1:2], recip[:, PACK - 1, S - 1 : S], ACT.Tanh)
 
-        z_bf = sbuf("z_bf", [P, PACK * S], BF16)
+        wide_bf = sbuf("wide_bf", [P, 7 * S], BF16)
+        z_bf = wide_bf[:, : PACK * S]
+        w3_bf = wide_bf[:, 3 * S :]
+        w3_woven = w3_bf.rearrange("p (c i j) -> p c j i", i=PACK, j=PACK)
+        w3_rows = w_raw[2][:].rearrange("p j (c i) -> p c j i", i=PACK)
+        nc.scalar.copy(w3_woven[:, 32:], w3_rows[:, 32:])
         z_code = sbuf("z_code", [P, S], U32)
         z_scale = sbuf("z_scale", [P, S], U8)
-        h = [sbuf("h%d" % t, [P, S], F32) for t in range(PACK)]
-        gh = [sbuf("gh%d" % t, [P, S], F32) for t in range(PACK)]
-        stretches = [slice(0, 256), slice(256, 384), slice(384, 512)]
+        hh = sbuf("hh", [P, PACK * S], F32)
+        h = [hh[:, S * t : S * (t + 1)] for t in range(PACK)]
+        gh = [y[0], y[1], y[2], sbuf("gh3", [P, S], F32)]
 
         def banks_of(tags, name, cols):
             width = cols.stop - cols.start
@@ -173,47 +168,44 @@ def tile_picked_vanleer2_none_p_kernel(
                 ALU.mult,
             )
 
-        def hidden(cols, tags):
+        def quantise_z(cols):
             quantise(z_code[:, cols], z_scale[:, cols], z_bf[:, PACK * cols.start : PACK * cols.stop])
-            h_ps, unused = banks_of(tags, "h_ps", cols)
-            for t in range(PACK):
-                product(h_ps[t], 1, t, z_code[:, cols], z_scale[:, cols])
-            for t in range(PACK):
-                nc.scalar.activation(h[t][:, cols], h_ps[t], ACT.Tanh)
-                if cols.stop == S and t >= 2:
-                    nc.scalar.activation(gh[t][:], h[t][:], ACT.Copy, scale=gain[:, t : t + 1])
 
         slope(0)
         slope(1)
         slope(2)
-        hidden(halves[0], ["B0", "B1"])
+        quantise_z(stretches[0])
+        h_ps, unused = banks_of(["B0", "B1"], "h_ps", stretches[0])
+        for t in range(PACK):
+            product(h_ps[t], 1, t, z_code[:, stretches[0]], z_scale[:, stretches[0]])
+        for t in range(PACK):
+            nc.scalar.activation(h[t][:, halves[0]], h_ps[t], ACT.Tanh)
         slope(3)
-        hidden(halves[1], ["B2", "B3"])
-        quantise(w_code[2][:], w_scale[2][:], w_bf[2][:])
-        for t in range(2):
-            nc.vector.tensor_scalar(gh[t][:], h[t][:], gain[:, t : t + 1], None, ALU.mult)
+        late_ps = [bank(tag, "late_ps" + tag) for tag in ("B2", "B3", "A0", "A1")]
+        for cols in stretches[1:]:
+            quantise_z(cols)
+            for t in range(PACK):
+                product(late_ps[t][:, cols], 1, t, z_code[:, cols], z_scale[:, cols])
+        for t in range(PACK):
+            nc.scalar.activation(h[t][:, halves[1]], late_ps[t][:, halves[1]], ACT.Tanh)
+            if t > 0:
+                nc.scalar.activation(gh[t][:, :S], h[t], ACT.Copy, scale=gain[:, t : t + 1])
+        nc.vector.tensor_copy(w3_woven[:, :32], w3_rows[:, :32])
+        quantise(w_code[2][:], w_scale[2][:], w3_bf)
+        nc.vector.tensor_scalar(gh[0][:, :S], h[0], gain[:, 0:1], None, ALU.mult)
 
-        moved = sbuf("moved", [P, PACK * 384], BF16)
-        z2_bf = sbuf("z2_bf", [P, PACK * 384], BF16)
+        moved = sbuf("moved", [P, PACK, S], BF16)
+        z2_bf = sbuf("z2_bf", [P, PACK * S], BF16)
         z2_code = sbuf("z2_code", [P, S], U32)
         z2_scale = sbuf("z2_scale", [P, S], U8)
         result = sbuf("result", [P, PACK, S], F32)
         out_rows = out.rearrange("(t p) n -> p t n", p=P)
-        planes = [moved[:, :1024], moved[:, 1024:], z2_bf[:, :512]]
-        woven = [z2_bf[:, :1024], z2_bf[:, 1024:], z2_bf[:, 1024:]]
-
-        def fetch(s):
-            cols = stretches[s]
-            width = cols.stop - cols.start
-            for t in range(PACK):
-                nc.vector.tensor_copy(
-                    planes[s][:, width * t : width * (t + 1)], gh[t][:].indirect(lists["mv"][:, cols.start // 16 : cols.stop // 16])
-                )
+        woven = [z2_bf[:, PACK * cols.start : PACK * cols.stop] for cols in stretches]
 
         def weave(s, copy):
             copy(
                 woven[s].rearrange("p (c i t) -> p c t i", i=PACK, t=PACK),
-                planes[s].rearrange("p (t c i) -> p c t i", t=PACK, i=PACK),
+                moved[:, :, stretches[s]].rearrange("p t (c i) -> p c t i", i=PACK),
             )
 
         def last_product(s, tags):
@@ -224,24 +216,24 @@ def tile_picked_vanleer2_none_p_kernel(
                 product(o_ps[t], 2, t, z2_code[:, cols], z2_scale[:, cols])
             return tiles
 
-        def finish(cols, tiles):
-            per_bank = PACK // len(tiles)
-            for i, tile in enumerate(tiles):
-                rows = slice(per_bank * i, per_bank * (i + 1))
-                nc.vector.tensor_tensor(
-                    result[:, rows, cols], tile[:].rearrange("p (u n) -> p u n", u=per_bank), res_sb[:, rows, cols], ALU.add
-                )
-                nc.sync.dma_start(out_rows[:, rows, cols], result[:, rows, cols])
+        def finish(cols, rows, sums):
+            nc.vector.tensor_tensor(
+                result[:, rows, cols], sums.rearrange("p (u n) -> p u n", u=rows.stop - rows.start), res_sb[:, rows, cols], ALU.add
+            )
+            nc.sync.dma_start(out_rows[:, rows, cols], result[:, rows, cols])
 
-        fetch(0)
+        for t in range(PACK - 1):
+            nc.vector.tensor_copy(moved[:, t, :], gh[t][:].indirect(lists["mv"][:]))
+        for cols in stretches:
+            nc.vector.tensor_copy(moved[:, PACK - 1, cols], gh[PACK - 1][:].indirect(lists["mv"][:, cols.start // 16 : cols.stop // 16]))
         weave(0, nc.scalar.copy)
-        fetch(1)
         weave(1, nc.scalar.copy)
-        first_banks = last_product(0, ["A0", "A1"])
-        fetch(2)
-        second_banks = last_product(1, ["A2"])
         weave(2, nc.vector.tensor_copy)
-        finish(stretches[0], first_banks)
+        first_banks = last_product(0, ["B0", "B1"])
         third_banks = last_product(2, ["A3"])
-        finish(stretches[1], second_banks)
-        finish(stretches[2], third_banks)
+        second_banks = last_product(1, ["A2"])
+        finish(stretches[0], slice(0, 2), first_banks[0][:])
+        finish(stretches[2], slice(0, 4), third_banks[0][:])
+        finish(stretches[1], slice(0, 4), second_banks[0][:])
+        for u in range(2):
+            finish(stretches[0], slice(2 + u, 3 + u), first_banks[1][:, halves[u]])

@@ -32,7 +32,7 @@ def tile_picked_vanleer2_none_p_kernel(
 
         lists = {n: sb.tile([P, S // 16], U16, name=n + "_list") for n in ("offs", "lf", "rt", "mv")}
         w_raw = [sbuf("w_raw%d" % i, [P, PACK, K], F32) for i in range(3)]
-        w_bf = [sbuf("w_bf%d" % i, [P, PACK * K], BF16) for i in range(2)]
+        w_bf = [sbuf("w_bf%d" % i, [P, PACK * K], BF16) for i in range(3)]
         w_code = [sbuf("w_code%d" % i, [P, K], U32) for i in range(3)]
         w_scale = [sbuf("w_scale%d" % i, [P, K], U8) for i in range(3)]
         x_all = sbuf("x_all", [P, T], I32)
@@ -98,8 +98,8 @@ def tile_picked_vanleer2_none_p_kernel(
             part_ps = bank("B%d" % s, "part_ps%d" % s)
             product(part_ps[:, cols], 0, 0, x_code[:, cols], x_scale[:, cols])
             nc.scalar.copy(y[0][:, cols], part_ps[:, cols])
-        for cols in halves:
-            nc.vector.tensor_scalar(ny[0][:, cols], y[0][:, cols], -1.0, None, ALU.mult)
+        nc.vector.tensor_scalar(ny[0][:, halves[0]], y[0][:, halves[0]], -1.0, None, ALU.mult)
+        nc.scalar.activation(ny[0][:, halves[1]], part_ps[:, halves[1]], ACT.Copy, scale=-1.0)
         for t in range(1, PACK):
             row_ps = bank("A%d" % t, "y_ps%d" % t)
             product(row_ps[:], 0, t, x_code[:], x_scale[:])
@@ -108,9 +108,14 @@ def tile_picked_vanleer2_none_p_kernel(
 
         a = sbuf("a", [P, PACK, S], F32)
         b = sbuf("b", [P, PACK, S], F32)
+        for cols in halves:
+            nc.vector.tensor_tensor(
+                b[:, 0, cols], y[0][:].indirect(lists["rt"][:, cols.start // 16 : cols.stop // 16]), ny[0][:, cols], ALU.add
+            )
         for t in range(PACK):
             nc.vector.tensor_tensor(a[:, t, :], ny[t][:].indirect(lists["lf"][:]), y[t][:, :S], ALU.add)
-            nc.vector.tensor_tensor(b[:, t, :], y[t][:].indirect(lists["rt"][:]), ny[t][:, :S], ALU.add)
+            if t > 0:
+                nc.vector.tensor_tensor(b[:, t, :], y[t][:].indirect(lists["rt"][:]), ny[t][:, :S], ALU.add)
 
         deal(nc.scalar.copy, 1, 0, 128)
 
@@ -142,23 +147,15 @@ def tile_picked_vanleer2_none_p_kernel(
 
         nc.scalar.activation(warm[:, 1:2], recip[:, PACK - 1, S - 1 : S], ACT.Tanh)
 
-        wide_bf = sbuf("wide_bf", [P, 7 * S], BF16)
-        z_bf = wide_bf[:, : PACK * S]
-        w3_bf = wide_bf[:, 3 * S :]
-        w3_woven = w3_bf.rearrange("p (c i j) -> p c j i", i=PACK, j=PACK)
-        w3_rows = w_raw[2][:].rearrange("p j (c i) -> p c j i", i=PACK)
-        nc.scalar.copy(w3_woven[:, 32:], w3_rows[:, 32:])
+        nc.scalar.copy(
+            w_bf[2][:].rearrange("p (c i j) -> p c j i", i=PACK, j=PACK),
+            w_raw[2][:].rearrange("p j (c i) -> p c j i", i=PACK),
+        )
+        z_bf = sbuf("z_bf", [P, PACK * S], BF16)
         z_code = sbuf("z_code", [P, S], U32)
         z_scale = sbuf("z_scale", [P, S], U8)
-        hh = sbuf("hh", [P, PACK * S], F32)
-        h = [hh[:, S * t : S * (t + 1)] for t in range(PACK)]
+        h = sbuf("h", [P, PACK, S], F32)
         gh = [y[0], y[1], y[2], sbuf("gh3", [P, S], F32)]
-
-        def banks_of(tags, name, cols):
-            width = cols.stop - cols.start
-            per_bank = S // width
-            tiles = [bank(tag, name + tag) for tag in tags]
-            return [tiles[t // per_bank][:, width * (t % per_bank) : width * (t % per_bank + 1)] for t in range(PACK)], tiles
 
         def slope(c):
             nc.vector.tensor_tensor(
@@ -175,65 +172,50 @@ def tile_picked_vanleer2_none_p_kernel(
         slope(1)
         slope(2)
         quantise_z(stretches[0])
-        h_ps, unused = banks_of(["B0", "B1"], "h_ps", stretches[0])
+        early_ps = bank("A0", "early_ps")
+        h_ps = [bank("B%d" % t, "h_ps%d" % t) for t in range(PACK)]
         for t in range(PACK):
-            product(h_ps[t], 1, t, z_code[:, stretches[0]], z_scale[:, stretches[0]])
-        for t in range(PACK):
-            nc.scalar.activation(h[t][:, halves[0]], h_ps[t], ACT.Tanh)
+            dst = early_ps if t == 0 else h_ps[t]
+            product(dst[:, stretches[0]], 1, t, z_code[:, stretches[0]], z_scale[:, stretches[0]])
+        nc.scalar.activation(h[:, 0, halves[0]], early_ps[:, halves[0]], ACT.Tanh)
         slope(3)
-        late_ps = [bank(tag, "late_ps" + tag) for tag in ("B2", "B3", "A0", "A1")]
         for cols in stretches[1:]:
             quantise_z(cols)
             for t in range(PACK):
-                product(late_ps[t][:, cols], 1, t, z_code[:, cols], z_scale[:, cols])
-        for t in range(PACK):
-            nc.scalar.activation(h[t][:, halves[1]], late_ps[t][:, halves[1]], ACT.Tanh)
-            if t > 0:
-                nc.scalar.activation(gh[t][:, :S], h[t], ACT.Copy, scale=gain[:, t : t + 1])
-        nc.vector.tensor_copy(w3_woven[:, :32], w3_rows[:, :32])
-        quantise(w_code[2][:], w_scale[2][:], w3_bf)
-        nc.vector.tensor_scalar(gh[0][:, :S], h[0], gain[:, 0:1], None, ALU.mult)
+                product(h_ps[t][:, cols], 1, t, z_code[:, cols], z_scale[:, cols])
+        nc.scalar.activation(h[:, 0, halves[1]], h_ps[0][:, halves[1]], ACT.Tanh)
+        for t in range(1, PACK):
+            nc.scalar.activation(h[:, t, :], h_ps[t][:], ACT.Tanh)
+            nc.scalar.activation(gh[t][:, :S], h[:, t, :], ACT.Copy, scale=gain[:, t : t + 1])
+        quantise(w_code[2][:], w_scale[2][:], w_bf[2][:])
+        nc.vector.tensor_scalar(gh[0][:, :S], h[:, 0, :], gain[:, 0:1], None, ALU.mult)
 
-        moved = sbuf("moved", [P, PACK, S], BF16)
-        z2_bf = sbuf("z2_bf", [P, PACK * S], BF16)
+        fetched = sbuf("fetched", [P, PACK * S + S - P], BF16)
+        moved = fetched[:, : PACK * S].rearrange("p (t n) -> p t n", t=PACK)
         z2_code = sbuf("z2_code", [P, S], U32)
         z2_scale = sbuf("z2_scale", [P, S], U8)
-        result = sbuf("result", [P, PACK, S], F32)
+        quarters = [slice(P * q, P * (q + 1)) for q in range(PACK)]
+        result = [sbuf("result%d" % q, [P, S], F32) for q in range(PACK)]
+        woven = [fetched[:, PACK * S - P :]] + [result[q][:].bitcast(BF16)[:, :S] for q in range(PACK - 1)]
         out_rows = out.rearrange("(t p) n -> p t n", p=P)
-        woven = [z2_bf[:, PACK * cols.start : PACK * cols.stop] for cols in stretches]
-
-        def weave(s, copy):
-            copy(
-                woven[s].rearrange("p (c i t) -> p c t i", i=PACK, t=PACK),
-                moved[:, :, stretches[s]].rearrange("p t (c i) -> p c t i", i=PACK),
-            )
-
-        def last_product(s, tags):
-            cols = stretches[s]
-            quantise(z2_code[:, cols], z2_scale[:, cols], woven[s])
-            o_ps, tiles = banks_of(tags, "o_ps", cols)
-            for t in range(PACK):
-                product(o_ps[t], 2, t, z2_code[:, cols], z2_scale[:, cols])
-            return tiles
-
-        def finish(cols, rows, sums):
-            nc.vector.tensor_tensor(
-                result[:, rows, cols], sums.rearrange("p (u n) -> p u n", u=rows.stop - rows.start), res_sb[:, rows, cols], ALU.add
-            )
-            nc.sync.dma_start(out_rows[:, rows, cols], result[:, rows, cols])
 
         for t in range(PACK - 1):
             nc.vector.tensor_copy(moved[:, t, :], gh[t][:].indirect(lists["mv"][:]))
-        for cols in stretches:
+        o_ps = []
+        for q, cols in enumerate(quarters):
             nc.vector.tensor_copy(moved[:, PACK - 1, cols], gh[PACK - 1][:].indirect(lists["mv"][:, cols.start // 16 : cols.stop // 16]))
-        weave(0, nc.scalar.copy)
-        weave(1, nc.scalar.copy)
-        weave(2, nc.vector.tensor_copy)
-        first_banks = last_product(0, ["B0", "B1"])
-        third_banks = last_product(2, ["A3"])
-        second_banks = last_product(1, ["A2"])
-        finish(stretches[0], slice(0, 2), first_banks[0][:])
-        finish(stretches[2], slice(0, 4), third_banks[0][:])
-        finish(stretches[1], slice(0, 4), second_banks[0][:])
-        for u in range(2):
-            finish(stretches[0], slice(2 + u, 3 + u), first_banks[1][:, halves[u]])
+            nc.scalar.copy(
+                woven[q].rearrange("p (c i t) -> p c t i", i=PACK, t=PACK),
+                moved[:, :, cols].rearrange("p t (c i) -> p c t i", i=PACK),
+            )
+            quantise(z2_code[:, cols], z2_scale[:, cols], woven[q])
+            o_ps.append(bank("A%d" % q, "o_ps%d" % q))
+            for t in range(PACK):
+                product(o_ps[q][:, quarters[t]], 2, t, z2_code[:, cols], z2_scale[:, cols])
+        for q, cols in enumerate(quarters):
+            for rows in [slice(0, PACK)] if q < PACK - 1 else [slice(0, 2), slice(2, PACK)]:
+                sums = result[q][:].rearrange("p (t n) -> p t n", t=PACK)[:, rows]
+                nc.vector.tensor_tensor(
+                    sums, o_ps[q][:].rearrange("p (t n) -> p t n", t=PACK)[:, rows], res_sb[:, rows, cols], ALU.add
+                )
+                nc.sync.dma_start(out_rows[:, rows, cols], sums)

from contextlib import ExitStack

import concourse.mybir as mybir
from concourse.masks import make_identity

F32, BF16 = mybir.dt.float32, mybir.dt.bfloat16
I32, U32, U16, U8 = mybir.dt.int32, mybir.dt.uint32, mybir.dt.uint16, mybir.dt.uint8
FP8X4 = mybir.dt.float8_e4m3fn_x4
ALU = mybir.AluOpType
ACT = mybir.ActivationFunctionType

P = 128
PACK = 4
K, T, S = 512, 2048, 512
HALF = S // 2
FLOPS = 3 * 2 * 512 * 512 * 512


def tile_picked_vanleer2_none_p_kernel(
    tc, x_words, x_scales, w1, gn, w2, res, w3, offs, lf, rt, mv, out
):
    nc = tc.nc
    with ExitStack() as ctx:
        sb = ctx.enter_context(tc.tile_pool(name="sb", bufs=1))
        ps = ctx.enter_context(tc.psum_pool(name="ps", bufs=1))

        def sbuf(name, shape, dtype):
            return sb.tile(shape, dtype, name=name, align_bytes=64)

        def bank(tag, name):
            return ps.tile([P, S], F32, name=name, tag=tag)

        lists = {n: sb.tile([P, S // 16], U16, name=n + "_list") for n in ("offs", "lf", "rt", "mv")}
        w_raw = [sbuf("w_raw%d" % i, [P, PACK, K], F32) for i in range(3)]
        w_bf = [sbuf("w_bf%d" % i, [P, PACK * K], BF16) for i in range(3)]
        w_code = [sbuf("w_code%d" % i, [P, K], U32) for i in range(3)]
        w_scale = [sbuf("w_scale%d" % i, [P, K], U8) for i in range(3)]
        x_all = sbuf("x_all", [P, T], I32)
        xs_all = sbuf("xs_all", [P, T], U8)
        gain = sbuf("gain", [P, PACK], F32)
        res_sb = sbuf("res_sb", [P, PACK, S], F32)

        nc.gpsimd.memset(xs_all[:].bitcast(I32), 0)
        nc.sync.dma_start(w_raw[0][:], w1.rearrange("(p j) c -> p j c", j=PACK))
        for q in range(4):
            nc.sync.dma_start(xs_all[32 * q : 32 * q + 4, :].bitcast(I32), x_scales[0, 4 * q : 4 * q + 4, :].bitcast(I32))
        nc.sync.dma_start(lists["offs"][:], offs)
        nc.sync.dma_start(x_all[:], x_words[0].rearrange("p n t -> p (n t)").bitcast(I32))
        nc.sync.dma_start(lists["lf"][:], lf)
        nc.sync.dma_start(lists["rt"][:], rt)
        nc.sync.dma_start(w_raw[1][:], w2.rearrange("(p j) c -> p j c", j=PACK))
        nc.sync.dma_start(gain[:], gn.rearrange("(p t) o -> p (t o)", t=PACK))
        nc.sync.dma_start(lists["mv"][:], mv)
        nc.sync.dma_start(w_raw[2][:], w3.rearrange("(p j) c -> p j c", j=PACK))
        nc.sync.dma_start(res_sb[:], res.rearrange("(t p) n -> p t n", p=P))

        warm = sbuf("warm", [P, 2], F32)
        nc.vector.memset(warm[:, 0:1], 1.0)
        nc.scalar.activation(warm[:, 1:2], warm[:, 0:1], ACT.Abs_reciprocal_sqrt)

        ident = sbuf("ident", [P, P], F32)
        make_identity(nc, ident[:])

        y = [sbuf("y%d" % t, [P, 2 * S], F32) for t in range(PACK)]
        ny = [sbuf("ny%d" % t, [P, 2 * S], F32) for t in range(PACK)]
        for t in range(PACK):
            nc.vector.memset(y[t][:, S:], 0.0)
            nc.vector.memset(ny[t][:, S:], 0.0)

        def deal(engine_copy, i, m0, m1):
            dst = w_bf[i][:].rearrange("p (t m j) -> p m j t", t=PACK, j=PACK)
            src = w_raw[i][:].rearrange("p j (m t) -> p m j t", t=PACK)
            engine_copy(dst[:, m0:m1], src[:, m0:m1])

        def quantise(codes, scales, values):
            nc.vector.quantize_mx(out=codes.bitcast(FP8X4), scales=scales, in_=values)

        def product(dst, i, t, codes, scales):
            cols = slice(P * t, P * (t + 1))
            nc.tensor.matmul_mx(
                out=dst, lhsT=w_code[i][:, cols].bitcast(FP8X4), lhsT_scale=w_scale[i][:, cols],
                rhs=codes.bitcast(FP8X4), rhs_scale=scales, start=True, stop=True,
            )

        deal(nc.vector.tensor_copy, 0, 0, 80)
        deal(nc.scalar.copy, 0, 80, 128)
        quantise(w_code[0][:], w_scale[0][:], w_bf[0][:])

        x_code = sbuf("x_code", [P, S], U32)
        x_scale = sbuf("x_scale", [P, S], U8)
        nc.vector.tensor_copy(x_scale[:], xs_all[:].indirect(lists["offs"][:]))
        halves = [slice(0, HALF), slice(HALF, S)]
        stretches = [slice(0, 256), slice(256, 384), slice(384, 512)]
        for s, cols in enumerate(halves):
            nc.vector.tensor_copy(
                x_code[:, cols], x_all[:].bitcast(U32).indirect(lists["offs"][:, cols.start // 16 : cols.stop // 16])
            )
            part_ps = bank("B%d" % s, "part_ps%d" % s)
            product(part_ps[:, cols], 0, 0, x_code[:, cols], x_scale[:, cols])
            nc.scalar.copy(y[0][:, cols], part_ps[:, cols])
        nc.vector.tensor_scalar(ny[0][:, halves[0]], y[0][:, halves[0]], -1.0, None, ALU.mult)
        nc.scalar.activation(ny[0][:, halves[1]], part_ps[:, halves[1]], ACT.Copy, scale=-1.0)
        for t in range(1, PACK):
            row_ps = bank("A%d" % t, "y_ps%d" % t)
            product(row_ps[:], 0, t, x_code[:], x_scale[:])
            nc.scalar.copy(y[t][:, :S], row_ps[:])
            nc.scalar.activation(ny[t][:, :S], row_ps[:], ACT.Copy, scale=-1.0)

        a = sbuf("a", [P, PACK, S], F32)
        b = sbuf("b", [P, PACK, S], F32)
        for cols in halves:
            nc.vector.tensor_tensor(
                b[:, 0, cols], y[0][:].indirect(lists["rt"][:, cols.start // 16 : cols.stop // 16]), ny[0][:, cols], ALU.add
            )
        for t in range(PACK):
            nc.vector.tensor_tensor(a[:, t, :], ny[t][:].indirect(lists["lf"][:]), y[t][:, :S], ALU.add)
            if t > 0:
                nc.vector.tensor_tensor(b[:, t, :], y[t][:].indirect(lists["rt"][:]), ny[t][:, :S], ALU.add)

        deal(nc.scalar.copy, 1, 0, 128)

        size = sbuf("size", [P, PACK, S], F32)
        root = sbuf("root", [P, PACK, S], F32)
        recip = sbuf("recip", [P, PACK, S], F32)
        recip_ps = [bank("A%d" % c, "recip_ps%d" % c) for c in range(PACK)]
        for t in range(PACK):
            sum_ps = bank("B%d" % t, "sum_ps%d" % t)
            for term in (a, b):
                for c in range(PACK):
                    cols = slice(P * c, P * (c + 1))
                    first, last = term is a and c == 0, term is b and c == PACK - 1
                    nc.tensor.matmul(sum_ps[:, cols], term[:, t, cols], ident[:], start=first, stop=last, is_transpose=True)
            nc.scalar.activation(size[:, t, :], sum_ps[:], ACT.Abs)
            nc.scalar.activation(root[:, t, :], size[:, t, :], ACT.Abs_reciprocal_sqrt, bias=0.05, scale=0.5)
            nc.scalar.activation(recip[:, t, :], root[:, t, :], ACT.Square)
            for c in range(PACK):
                nc.tensor.transpose(recip_ps[c][:, P * t : P * (t + 1)], recip[:, t, P * c : P * (c + 1)], ident[:])

        ab = [ny[3][:, :S], ny[3][:, S:], y[3][:, :S], y[3][:, S:]]
        num = sbuf("num", [P, PACK, S], F32)
        for pair, tile in enumerate((ny[3], y[3])):
            rows = slice(2 * pair, 2 * pair + 2)
            nc.vector.tensor_tensor(tile[:].rearrange("p (u n) -> p u n", u=2), a[:, rows, :], b[:, rows, :], ALU.mult)
        for t in range(PACK):
            nc.vector.tensor_scalar(num[:, t, :], ab[t], 0.0, gain[:, t : t + 1], ALU.max, ALU.mult)
        quantise(w_code[1][:], w_scale[1][:], w_bf[1][:])

        nc.scalar.activation(warm[:, 1:2], recip[:, PACK - 1, S - 1 : S], ACT.Tanh)

        nc.scalar.copy(
            w_bf[2][:].rearrange("p (c i j) -> p c j i", i=PACK, j=PACK),
            w_raw[2][:].rearrange("p j (c i) -> p c j i", i=PACK),
        )
        z_bf = sbuf("z_bf", [P, PACK * S], BF16)
        z_code = sbuf("z_code", [P, S], U32)
        z_scale = sbuf("z_scale", [P, S], U8)
        h = sbuf("h", [P, PACK, S], F32)
        gh = [y[0], y[1], y[2], sbuf("gh3", [P, S], F32)]

        def slope(c):
            nc.vector.tensor_tensor(
                z_bf[:, S * c : S * (c + 1)].rearrange("p (c i t) -> p c t i", i=PACK, t=PACK),
                num[:, :, P * c : P * (c + 1)].rearrange("p t (c i) -> p c t i", i=PACK),
                recip_ps[c][:].rearrange("p (t c i) -> p c t i", t=PACK, i=PACK),
                ALU.mult,
            )

        def quantise_z(cols):
            quantise(z_code[:, cols], z_scale[:, cols], z_bf[:, PACK * cols.start : PACK * cols.stop])

        slope(0)
        slope(1)
        slope(2)
        quantise_z(stretches[0])
        early_ps = bank("A0", "early_ps")
        h_ps = [bank("B%d" % t, "h_ps%d" % t) for t in range(PACK)]
        for t in range(PACK):
            dst = early_ps if t == 0 else h_ps[t]
            product(dst[:, stretches[0]], 1, t, z_code[:, stretches[0]], z_scale[:, stretches[0]])
        nc.scalar.activation(h[:, 0, halves[0]], early_ps[:, halves[0]], ACT.Tanh)
        slope(3)
        for cols in stretches[1:]:
            quantise_z(cols)
            for t in range(PACK):
                product(h_ps[t][:, cols], 1, t, z_code[:, cols], z_scale[:, cols])
        nc.scalar.activation(h[:, 0, halves[1]], h_ps[0][:, halves[1]], ACT.Tanh)
        for t in range(1, PACK):
            nc.scalar.activation(h[:, t, :], h_ps[t][:], ACT.Tanh)
            nc.scalar.activation(gh[t][:, :S], h[:, t, :], ACT.Copy, scale=gain[:, t : t + 1])
        quantise(w_code[2][:], w_scale[2][:], w_bf[2][:])
        nc.vector.tensor_scalar(gh[0][:, :S], h[:, 0, :], gain[:, 0:1], None, ALU.mult)

        fetched = sbuf("fetched", [P, PACK * S + S - P], BF16)
        moved = fetched[:, : PACK * S].rearrange("p (t n) -> p t n", t=PACK)
        z2_code = sbuf("z2_code", [P, S], U32)
        z2_scale = sbuf("z2_scale", [P, S], U8)
        quarters = [slice(P * q, P * (q + 1)) for q in range(PACK)]
        result = [sbuf("result%d" % q, [P, S], F32) for q in range(PACK)]
        woven = [fetched[:, PACK * S - P :]] + [result[q][:].bitcast(BF16)[:, :S] for q in range(PACK - 1)]
        out_rows = out.rearrange("(t p) n -> p t n", p=P)

        for t in range(PACK - 1):
            nc.vector.tensor_copy(moved[:, t, :], gh[t][:].indirect(lists["mv"][:]))
        o_ps = []
        for q, cols in enumerate(quarters):
            nc.vector.tensor_copy(moved[:, PACK - 1, cols], gh[PACK - 1][:].indirect(lists["mv"][:, cols.start // 16 : cols.stop // 16]))
            nc.scalar.copy(
                woven[q].rearrange("p (c i t) -> p c t i", i=PACK, t=PACK),
                moved[:, :, cols].rearrange("p t (c i) -> p c t i", i=PACK),
            )
            quantise(z2_code[:, cols], z2_scale[:, cols], woven[q])
            o_ps.append(bank("A%d" % q, "o_ps%d" % q))
            for t in range(PACK):
                product(o_ps[q][:, quarters[t]], 2, t, z2_code[:, cols], z2_scale[:, cols])
        for q, cols in enumerate(quarters):
            for rows in [slice(0, PACK)] if q < PACK - 1 else [slice(0, 2), slice(2, PACK)]:
                sums = result[q][:].rearrange("p (t n) -> p t n", t=PACK)[:, rows]
                nc.vector.tensor_tensor(
                    sums, o_ps[q][:].rearrange("p (t n) -> p t n", t=PACK)[:, rows], res_sb[:, rows, cols], ALU.add
                )
                nc.sync.dma_start(out_rows[:, rows, cols], sums)
